import numpy as np
import ml_dtypes


def mxq(x, axis, fmt="e4m3"):
    dtype, down = {"e4m3": (ml_dtypes.float8_e4m3fn, 7), "e5m2": (ml_dtypes.float8_e5m2, 14)}[fmt]
    v = np.moveaxis(np.asarray(x, np.float32).astype(ml_dtypes.bfloat16).astype(np.float64), axis, -1)
    blocks = v.reshape(v.shape[:-1] + (-1, 32))
    amax = np.abs(blocks).max(-1, keepdims=True)
    byte = np.maximum(np.where(amax > 0, np.frexp(amax)[1] - 1 + 127, 0) - down, 1)
    scale = np.exp2(byte - 127.0)
    codes = (blocks / scale).astype(np.float32).astype(dtype).astype(np.float64)
    return np.moveaxis((codes * scale).reshape(v.shape), -1, axis)


WIDE = False


def mx_kscale(k):
    if not WIDE:
        return np.ones(k)
    levels = np.array([10, -10, 5, -5, 0])
    if k % 512:
        return np.exp2(np.random.permutation(np.resize(levels, k // 32))).repeat(32)
    a = np.empty((k // 512, 16))
    for p in range(k // 512):
        a[p, :8] = np.random.permutation(np.resize(levels, 8))
        for g in range(8):
            far = levels[np.abs(levels - a[p, g]) >= 10]
            a[p, g + 8] = far[np.random.randint(len(far))]
    return np.exp2(a.ravel()).repeat(32)


def f64(x):
    return np.asarray(x).astype(np.float64)


def striped(idx):
    return np.tile(idx.reshape(-1, 16).T, (8, 1)).astype(np.uint16)


def unstriped(offs):
    return offs[:16].T.reshape(-1).astype(np.int64)


E2M1 = np.array([0.0, 0.5, 1.0, 1.5, 2.0, 3.0, 4.0, 6.0, -0.0, -0.5, -1.0, -1.5, -2.0, -3.0, -4.0, -6.0])


def pack_weight(w, fmt):
    k, n = w.shape
    w = f64(np.asarray(w, np.float32).astype(ml_dtypes.bfloat16)).reshape(k // 32, 32, n)
    amax = np.abs(w).max(1)
    if fmt == "e4m3":
        byte = np.frexp(amax)[1] - 1 + 127 - 7
    else:
        mant, ex = np.frexp(amax / 6.0)
        byte = np.where(mant > 0.5, ex, ex - 1) + 127
    byte = np.clip(np.where(amax > 0, byte, 1), 1, 254)
    scaled = (w * np.exp2(127.0 - byte)[:, None, :]).reshape(k, n).astype(np.float32)
    by_word = np.ascontiguousarray(scaled.reshape(k // 512, 128, 4, n).transpose(0, 1, 3, 2))
    if fmt == "e4m3":
        words = by_word.astype(ml_dtypes.float8_e4m3fn).view(np.uint8)
    else:
        c = by_word.astype(ml_dtypes.float4_e2m1fn).view(np.uint8) & 0xF
        words = (c[..., 0::2] | (c[..., 1::2] << 4)).reshape(k // 512, 128, 2 * n)
    return np.ascontiguousarray(words), np.ascontiguousarray(byte.astype(np.uint8).reshape(k // 512, 16, n))


def unpack_weight(words, scales, fmt):
    g, _, n = scales.shape
    words = np.ascontiguousarray(words).reshape(g, 128, n, -1)
    if fmt == "e4m3":
        vals = words.view(ml_dtypes.float8_e4m3fn).astype(np.float64)
    else:
        nib = np.empty((g, 128, n, 4), np.uint8)
        nib[..., 0::2] = words & 0xF
        nib[..., 1::2] = words >> 4
        vals = E2M1[nib]
    vals = vals * np.repeat(np.exp2(scales.astype(np.float64) - 127.0), 8, axis=1)[..., None]
    return vals.transpose(0, 1, 3, 2).reshape(g * 512, n)


def gelu(v):
    return 0.5 * v * (1.0 + np.tanh(np.sqrt(2.0 / np.pi) * (v + 0.044715 * v**3)))


T, S, T2, P, K, H, N = 4096, 1024, 2048, 512, 1024, 1024, 384

def setup_inputs():
    n = np.random.standard_normal
    s = mx_kscale(K)[:, None]
    u = mx_kscale(H)[:, None]
    tab_words, tab_scales = pack_weight(n((K, T)) * s, "e4m3")
    w4_words, w4_scales = pack_weight(0.48 * n((H, N)) / np.sqrt(H) / u, "e2m1")
    perm = np.random.permutation(T2)
    return {
        "tab_words": tab_words, "tab_scales": tab_scales,
        "offs": striped(np.random.permutation(T)[:S]),
        "offs2": striped(np.random.permutation(T2)[:S]),
        "offs3": striped(perm[:P]),
        "offs4": striped(perm[P:2 * P]),
        "w1": (0.5 * n((K, H)) / np.sqrt(K) / s).astype(np.float32),
        "gain": (np.random.uniform(0.6, 1.3, H) * u[:, 0]).astype(np.float32),
        "wgs": np.exp(0.3 * n((128, S))).astype(np.float32),
        "page0": (n((H, T2)) * u).astype(np.float32),
        "trade": np.random.uniform(0.5, 1.4, H).astype(np.float32),
        "shift": (0.5 * n(H) * u[:, 0]).astype(np.float32),
        "w4_words": w4_words, "w4_scales": w4_scales,
        "w2": (0.48 * n((H, N)) / np.sqrt(H) / u).astype(np.float32),
    }

def reference(tab_words, tab_scales, offs, offs2, offs3, offs4, w1, gain, wgs, page0, trade, shift, w4_words, w4_scales, w2):
    v = unpack_weight(tab_words, tab_scales, "e4m3")[:, unstriped(offs)]
    w4 = unpack_weight(w4_words, w4_scales, "e2m1")
    h = np.cos(mxq(f64(w1), 0, "e4m3").T @ v) * f64(gain)[:, None]
    page = f64(page0).copy()
    page[:, unstriped(offs2)] = np.tile(f64(wgs), (H // 128, 1)) * h
    a = page[:, unstriped(offs3)]
    b = page[:, unstriped(offs4)]
    page[:, unstriped(offs3)] = f64(trade)[:, None] * b
    page[:, unstriped(offs4)] = a + f64(shift)[:, None]
    pq = mxq(page, 0, "e4m3")
    y1 = w4.T @ pq
    y2 = mxq(f64(w2), 0, "e4m3").T @ pq
    return np.sin(y1) * np.cos(y2)

@@ -1,0 +1,354 @@
+import math
+from contextlib import ExitStack
+
+import concourse.mybir as mybir
+from concourse.masks import make_identity
+
+T, S, T2, PAIRS, K, H, N = 4096, 1024, 2048, 512, 1024, 1024, 384
+FLOPS = 2 * K * H * S + 2 * 2 * H * N * T2
+
+F32 = mybir.dt.float32
+BF16 = mybir.dt.bfloat16
+I32 = mybir.dt.int32
+U32 = mybir.dt.uint32
+U16 = mybir.dt.uint16
+U8 = mybir.dt.uint8
+E4M3X4 = mybir.dt.float8_e4m3fn_x4
+E2M1X4 = mybir.dt.float4_e2m1fn_x4
+ACT = mybir.ActivationFunctionType
+ALU = mybir.AluOpType
+
+P = 128
+PACK = 4
+PASS = P * PACK
+BANK = 512
+TURN = 2.0 * math.pi
+QUARTER = 0.25
+ALIGN = 64
+
+
+def tile_list_swipe_swap_scores_kernel(
+    tc, tab_words, tab_scales, offs, offs2, offs3, offs4, w1, gain, wgs, page0, trade, shift, w4_words, w4_scales, w2, out
+):
+    nc = tc.nc
+    slices = [(a, t) for a in range(H // PASS) for t in range(PACK)]
+    chunks = range(T2 // BANK)
+    halves = range(S // BANK)
+
+    with ExitStack() as ctx:
+        keep = ctx.enter_context(tc.tile_pool(name="keep", bufs=1))
+        big = ctx.enter_context(tc.tile_pool(name="big", bufs=2))
+        two = ctx.enter_context(tc.tile_pool(name="two", bufs=2))
+        four = ctx.enter_context(tc.tile_pool(name="four", bufs=4))
+        five = ctx.enter_context(tc.tile_pool(name="six", bufs=6))
+        eight = ctx.enter_context(tc.tile_pool(name="eight", bufs=8))
+        with tc.tile_pool(name="early", bufs=2) as early, tc.tile_pool(name="early1", bufs=1) as early1:
+
+            def load_list(src, name):
+                lst = keep.tile(list(src.shape), U16, name=name)
+                nc.sync.dma_start(lst[:], src)
+                return lst
+
+            def load_rows(src, name):
+                col = keep.tile([P, H // PASS, PACK], F32, name=name)
+                nc.sync.dma_start(out=col[:], in_=src.rearrange("(a p t) -> p a t", p=P, t=PACK))
+                return col
+
+            def load_weight(w, g, cols):
+                width = cols.stop - cols.start
+                raw = early.tile([P, PACK, width], F32, name="raw")
+                nc.sync.dma_start(out=raw[:], in_=w[g * PASS : (g + 1) * PASS, cols].rearrange("(p j) c -> p j c", j=PACK))
+                return raw
+
+            def quantize(grouped, width, pool, name):
+                codes = pool.tile([P, width], U32, name=name + "_codes", align_bytes=ALIGN)
+                scales = pool.tile([P, width], U8, name=name + "_scales", align_bytes=ALIGN)
+                nc.vector.quantize_mx(out=codes[:].bitcast(E4M3X4), scales=scales[:], in_=grouped)
+                return codes, scales
+
+            def quantize_w1(raw, a, g):
+                grouped = four.tile([P, PASS * PACK], BF16, name="woven", align_bytes=ALIGN)
+                nc.scalar.copy(
+                    out=grouped[:].rearrange("p (t m j) -> p m j t", t=PACK, j=PACK),
+                    in_=raw[:].rearrange("p j (m t) -> p m j t", t=PACK),
+                )
+                return quantize(grouped[:], PASS, eight, "mx")
+
+            def quantize_w2(raw, a):
+                grouped = four.tile([P, N * PACK], BF16, name="woven", align_bytes=ALIGN)
+                nc.scalar.copy(
+                    out=grouped[:].rearrange("p (c i j) -> p c j i", i=PACK, j=PACK),
+                    in_=raw[:].rearrange("p j (c i) -> p c j i", i=PACK),
+                )
+                return quantize(grouped[:], N, two, "w2")
+
+            def load_table_words(g):
+                words = big.tile([P, T], I32, name="big")
+                nc.sync.dma_start(out=words[:], in_=tab_words[g].rearrange("p n i -> p (n i)").bitcast(I32))
+                return words
+
+            def gather_table(src, dtype, name):
+                picked = []
+                for h in halves:
+                    part = early1.tile([P, BANK], dtype, name="%s_%d" % (name, h), align_bytes=ALIGN)
+                    cols = slice(h * BANK // 16, (h + 1) * BANK // 16)
+                    nc.vector.tensor_copy(part[:], src.indirect(list1[:, cols]))
+                    picked.append(part)
+                return picked
+
+            def load_wgs(t):
+                dealt = early1.tile([P, S], F32, name="wgs_%d" % t)
+                rows = wgs.rearrange("(q t) j -> t q j", t=PACK)[t]
+                for quad in range(4):
+                    nc.sync.dma_start(out=dealt[32 * quad : 32 * (quad + 1), :], in_=rows)
+                return dealt
+
+            def load_page(a, t):
+                page = five.tile([P, T2], F32, name="page")
+                rows = page0[a * PASS : (a + 1) * PASS, :].rearrange("(p t) c -> t p c", t=PACK)[t]
+                nc.sync.dma_start(out=page[:], in_=rows)
+                return page
+
+            table_scales = early1.tile([P, T], U8, name="table_scales")
+            nc.vector.memset(table_scales[:].bitcast(I32), 0)
+            ident = keep.tile([P, P], F32, name="ident")
+            make_identity(nc, ident[:])
+            ones = keep.tile([P, PAIRS], F32, name="ones")
+            nc.gpsimd.memset(ones[:], 1.0)
+            w4_plane = keep.tile([P, H // PASS, N], U8, name="w4_plane", align_bytes=ALIGN)
+            nc.gpsimd.memset(w4_plane[:].rearrange("p a n -> p (a n)").bitcast(I32), 0)
+
+            list1 = load_list(offs, "list1")
+            w1q = {}
+            raw = load_weight(w1, 0, slice(0, PASS))
+            w1q[0, 0] = quantize_w1(raw, 0, 0)
+            words0 = load_table_words(0)
+            for quad in range(4):
+                nc.sync.dma_start(
+                    out=table_scales[32 * quad : 32 * quad + 8, :].bitcast(I32),
+                    in_=tab_scales[:, 4 * quad : 4 * quad + 4, :].bitcast(I32),
+                )
+            raw = load_weight(w1, 1, slice(0, PASS))
+            w1q[0, 1] = quantize_w1(raw, 0, 1)
+            words1 = load_table_words(1)
+            v_codes = [gather_table(words0[:].bitcast(U32), U32, "v0")]
+            v_scales = gather_table(table_scales[:], U8, "vs")
+            v_codes.append(gather_table(words1[:].bitcast(U32), U32, "v1"))
+
+            gain_col = load_rows(gain, "gain_col")
+            list2 = load_list(offs2, "list2")
+            dealt = {0: load_wgs(0)}
+            pages = {0: load_page(*slices[0])}
+            list3 = load_list(offs3, "list3")
+            list4 = load_list(offs4, "list4")
+            trade_col = load_rows(trade, "trade_col")
+            shift_col = load_rows(shift, "shift_col")
+            raws = {}
+            for s in range(1, PACK):
+                pages[s] = load_page(*slices[s])
+                dealt[s] = load_wgs(s)
+            for g in range(K // PASS):
+                raws[g] = load_weight(w1, g, slice(PASS, 2 * PASS))
+            pages[PACK] = load_page(*slices[PACK])
+            pages[PACK + 1] = load_page(*slices[PACK + 1])
+            w4_codes = keep.tile([P, H // PASS, 2 * N], U8, name="w4_codes", align_bytes=ALIGN)
+            nc.sync.dma_start(out=w4_codes[:].bitcast(I32), in_=w4_words.bitcast(I32).rearrange("a p w -> p a w"))
+            for quad in range(4):
+                nc.sync.dma_start(
+                    out=w4_plane[32 * quad : 32 * quad + 4, :, :].bitcast(I32),
+                    in_=w4_scales[:, 4 * quad : 4 * quad + 4, :].bitcast(I32).rearrange("a q w -> q a w"),
+                )
+
+            def whole_turns(turns, size):
+                nc.scalar.activation(out=turns, in_=size[:], func=ACT.Copy, scale=1.0 / TURN, bias=QUARTER)
+
+            def reduce_on_vector(angle, turns, y, phase):
+                nc.vector.tensor_scalar(turns, y[:], 1.0 / TURN, phase, ALU.mult, ALU.add)
+                nc.vector.scalar_tensor_tensor(angle, turns, -TURN, y[:], ALU.mult, ALU.add)
+
+            def features(psum, s):
+                a, t = slices[s]
+                feature = two.tile([P, S], F32, name="feature")
+                turns = two.tile([P, S], U32, name="turns", align_bytes=ALIGN)
+                cosine = two.tile([P, S], F32, name="cosine", align_bytes=ALIGN)
+                spent = []
+                for h in halves:
+                    half = slice(h * BANK, (h + 1) * BANK)
+                    xt = psum.tile([P, BANK], F32, name="xt")
+                    for i in range(BANK // P):
+                        cols = slice(i * P, (i + 1) * P)
+                        for g in range(K // PASS):
+                            codes, scales = w1q[a, g]
+                            nc.tensor.matmul_mx(
+                                out=xt[:, cols],
+                                lhsT=v_codes[g][h][:, cols].bitcast(E4M3X4),
+                                lhsT_scale=v_scales[h][4 * g :, cols],
+                                rhs=codes[:, t * P : (t + 1) * P].bitcast(E4M3X4),
+                                rhs_scale=scales[:, t * P : (t + 1) * P],
+                                start=(g == 0),
+                                stop=(g == K // PASS - 1),
+                            )
+                    size = five.tile([P, BANK], F32, name="size")
+                    nc.scalar.activation(out=size[:], in_=xt[:], func=ACT.Abs)
+                    whole_turns(turns[:, half], size)
+                    back = five.tile([P, BANK], F32, name="back")
+                    nc.scalar.activation(out=back[:], in_=turns[:, half], func=ACT.Copy, scale=-TURN)
+                    angle = psum.tile([P, BANK], F32, name="angle")
+                    for i in range(BANK // P):
+                        cols = slice(i * P, (i + 1) * P)
+                        nc.tensor.matmul(angle[:, cols], size[:, cols], ident[:], start=True, stop=False, is_transpose=True)
+                        nc.tensor.matmul(angle[:, cols], back[:, cols], ident[:], start=False, stop=True, is_transpose=True)
+                    nc.scalar.activation(out=cosine[:, half], in_=angle[:], func=ACT.Sin, bias=TURN * QUARTER)
+                    nc.scalar.activation(
+                        out=feature[:, half], in_=cosine[:, half], func=ACT.Copy, scale=gain_col[:, a, t : t + 1]
+                    )
+                    spent.extend([size, back])
+                return feature, spent, [turns[:].bitcast(BF16), cosine[:].bitcast(BF16)]
+
+            def first_features(psum):
+                feature = two.tile([P, S], F32, name="feature")
+                turns = two.tile([P, S], I32, name="turns", align_bytes=ALIGN)
+                cosine = two.tile([P, S], F32, name="cosine", align_bytes=ALIGN)
+                for h in halves:
+                    half = slice(h * BANK, (h + 1) * BANK)
+                    x = psum.tile([P, BANK], F32, name="xt")
+                    for g in range(K // PASS):
+                        codes, scales = w1q[0, g]
+                        nc.tensor.matmul_mx(
+                            out=x[:],
+                            lhsT=codes[:, 0:P].bitcast(E4M3X4),
+                            lhsT_scale=scales[:, 0:P],
+                            rhs=v_codes[g][h][:].bitcast(E4M3X4),
+                            rhs_scale=v_scales[h][4 * g :, :],
+                            start=(g == 0),
+                            stop=(g == K // PASS - 1),
+                        )
+                    angle = five.tile([P, BANK], F32, name="size")
+                    reduce_on_vector(angle[:], turns[:, half], x, QUARTER)
+                    nc.scalar.activation(out=feature[:, half], in_=angle[:], func=ACT.Sin, bias=TURN * QUARTER)
+                nc.scalar.activation(out=cosine[:], in_=dealt[0][:], func=ACT.Copy, scale=gain_col[:, 0, 0:1])
+                return feature, cosine
+
+            def spread(wide, col, s):
+                a, t = slices[s]
+                nc.scalar.activation(out=wide, in_=ones[:], func=ACT.Copy, scale=col[:, a, t : t + 1])
+                return wide
+
+            def place(page, cosine, weight):
+                for h in halves:
+                    cols = slice(h * BANK, (h + 1) * BANK)
+                    entries = list2[:, h * BANK // 16 : (h + 1) * BANK // 16]
+                    nc.vector.tensor_tensor(page[:].indirect(entries), cosine[:, cols], weight[:, cols], ALU.mult)
+
+            def exchange(page, traded, shifted, first, second):
+                nc.vector.tensor_copy(second, page[:].indirect(list4[:]))
+                nc.vector.tensor_copy(first, page[:].indirect(list3[:]))
+                nc.vector.tensor_tensor(page[:].indirect(list3[:]), second, traded, ALU.mult)
+                nc.vector.tensor_tensor(page[:].indirect(list4[:]), first, shifted, ALU.add)
+
+            def park(page, parked, t):
+                for u, part in enumerate(parked):
+                    nc.sync.dma_start(out=part[:, t, :], in_=page[:, u * T2 // 2 : (u + 1) * T2 // 2])
+
+            def weave(woven, parked, c, planes):
+                src = parked[c // 2][:, 0:planes, (c % 2) * BANK : (c % 2 + 1) * BANK]
+                nc.scalar.copy(
+                    out=woven.rearrange("p (c i t) -> p c t i", i=PACK, t=PACK)[:, :, 0:planes, :],
+                    in_=src.rearrange("p t (c i) -> p c t i", i=PACK),
+                )
+                return woven
+
+            def weave_plane(copy, woven, page, c, t):
+                copy(
+                    out=woven[:].rearrange("p (c t) -> p c t", t=PACK)[:, :, t], in_=page[:, c * BANK : (c + 1) * BANK]
+                )
+
+            page_q = {}
+            w2q = {}
+            last = len(slices) - 1
+            with tc.psum_pool(name="stage1", bufs=2) as psum:
+                place(pages[0], *first_features(psum))
+                parked = {}
+                for s, (a, t) in enumerate(slices):
+                    if s < last - 1:
+                        feature, spent, free = features(psum, s + 1)
+                        place(pages[s + 1], feature, dealt[(s + 1) % PACK])
+                        spent = [tile[:] for tile in spent]
+                    else:
+                        spent = [five.tile([P, BANK], F32, name=name)[:] for name in ("size", "back", "size", "back")[2 * (s - last + 1) :]]
+                    if s < K // PASS:
+                        w1q[1, s] = quantize_w1(raws[s], 1, s)
+                    elif s < PACK:
+                        w2q[s - 2] = quantize_w2(load_weight(w2, s - 2, slice(0, N)), s - 2)
+                    if s == last - 2:
+                        for c, woven in enumerate(free):
+                            page_q[0, c] = quantize(weave(woven, parked[0], c, PACK), BANK, eight, "mx")
+                    if s == last:
+                        feature, unused, free = features(psum, s)
+                        for u, woven in enumerate(free):
+                            page_q[0, 2 + u] = quantize(weave(woven, parked[0], 2 + u, PACK), BANK, eight, "mx")
+                        place(pages[s], feature, dealt[t])
+                        woven_last = [four.tile([P, BANK * PACK], BF16, name="woven", align_bytes=ALIGN) for c in chunks]
+                        for c in chunks:
+                            weave(woven_last[c][:], parked[1], c, PACK - 1)
+                        spent = [part[:, 0, BANK // 2 : 3 * BANK // 2] for part in parked[1]] + spent
+                    traded, shifted = spread(spent[0], trade_col, s), spread(spent[1], shift_col, s)
+                    exchange(pages[s], traded, shifted, spent[2], spent[3])
+                    if s < last:
+                        if t == 0:
+                            parked[a] = [big.tile([P, PACK, T2 // 2], F32, name="big") for u in range(2)]
+                        park(pages[s], parked[a], t)
+                        if s + 6 <= last:
+                            pages[s + 6] = load_page(*slices[s + 6])
+
+        with tc.psum_pool(name="stage2", bufs=4) as psum, tc.tile_pool(name="three", bufs=4) as three:
+
+            def finish(c):
+                weave_plane(nc.scalar.copy if c in (1, 2) else nc.vector.tensor_copy, woven_last[c], pages[last], c, PACK - 1)
+                page_q[1, c] = quantize(woven_last[c][:], BANK, eight, "mx")
+
+            finish(0)
+            for c in chunks:
+                if c + 1 in chunks:
+                    finish(c + 1)
+                for i in range(N // P):
+                    cols = slice(i * P, (i + 1) * P)
+                    y1 = psum.tile([P, BANK], F32, name="y1")
+                    y2 = psum.tile([P, BANK], F32, name="y2")
+                    for a in range(H // PASS):
+                        codes, scales = page_q[a, c]
+                        nc.tensor.matmul_mx(
+                            out=y1[:],
+                            lhsT=w4_codes[:, a, 2 * i * P : 2 * (i + 1) * P].bitcast(E2M1X4),
+                            lhsT_scale=w4_plane[:, a, cols],
+                            rhs=codes[:].bitcast(E4M3X4),
+                            rhs_scale=scales[:],
+                            start=(a == 0),
+                            stop=(a == H // PASS - 1),
+                        )
+                        nc.tensor.matmul_mx(
+                            out=y2[:],
+                            lhsT=w2q[a][0][:, cols].bitcast(E4M3X4),
+                            lhsT_scale=w2q[a][1][:, cols],
+                            rhs=codes[:].bitcast(E4M3X4),
+                            rhs_scale=scales[:],
+                            start=(a == 0),
+                            stop=(a == H // PASS - 1),
+                        )
+                    turns1 = three.tile([P, BANK], I32, name="turns1")
+                    nc.vector.tensor_scalar(turns1[:], y1[:], 1.0 / TURN, None, ALU.mult)
+                    angle1 = three.tile([P, BANK], F32, name="angle1")
+                    nc.vector.scalar_tensor_tensor(angle1[:], turns1[:], -TURN, y1[:], ALU.mult, ALU.add)
+                    sine = three.tile([P, BANK], F32, name="sine")
+                    nc.scalar.activation(out=sine[:], in_=angle1[:], func=ACT.Sin)
+                    size = five.tile([P, BANK], F32, name="size")
+                    nc.scalar.activation(out=size[:], in_=y2[:], func=ACT.Abs)
+                    turns2 = three.tile([P, BANK], U32, name="turns2")
+                    whole_turns(turns2[:], size)
+                    angle2 = five.tile([P, BANK], F32, name="back")
+                    nc.vector.scalar_tensor_tensor(angle2[:], turns2[:].bitcast(I32), -TURN, size[:], ALU.mult, ALU.add)
+                    cos2 = three.tile([P, BANK], F32, name="cos2")
+                    nc.scalar.activation(out=cos2[:], in_=angle2[:], func=ACT.Sin, bias=TURN * QUARTER)
+                    score = three.tile([P, BANK], F32, name="score")
+                    nc.vector.tensor_tensor(score[:], sine[:], cos2[:], ALU.mult)
+                    nc.sync.dma_start(out=out[cols, c * BANK : (c + 1) * BANK], in_=score[:])

@@ -54,9 +54,9 @@ def tile_list_swipe_swap_scores_kernel(
                 nc.sync.dma_start(out=col[:], in_=src.rearrange("(a p t) -> p a t", p=P, t=PACK))
                 return col
 
-            def load_weight(w, g, cols):
+            def load_weight(w, g, cols, name):
                 width = cols.stop - cols.start
-                raw = early.tile([P, PACK, width], F32, name="raw")
+                raw = early.tile([P, PACK, width], F32, name=name)
                 nc.sync.dma_start(out=raw[:], in_=w[g * PASS : (g + 1) * PASS, cols].rearrange("(p j) c -> p j c", j=PACK))
                 return raw
 
@@ -66,21 +66,19 @@ def tile_list_swipe_swap_scores_kernel(
                 nc.vector.quantize_mx(out=codes[:].bitcast(E4M3X4), scales=scales[:], in_=grouped)
                 return codes, scales
 
-            def quantize_w1(raw, a, g):
-                grouped = four.tile([P, PASS * PACK], BF16, name="woven", align_bytes=ALIGN)
-                nc.scalar.copy(
-                    out=grouped[:].rearrange("p (t m j) -> p m j t", t=PACK, j=PACK),
+            def quantize_w1(copy, grouped, raw):
+                copy(
+                    out=grouped.rearrange("p (t m j) -> p m j t", t=PACK, j=PACK),
                     in_=raw[:].rearrange("p j (m t) -> p m j t", t=PACK),
                 )
-                return quantize(grouped[:], PASS, eight, "mx")
+                return quantize(grouped, PASS, eight, "mx")
 
-            def quantize_w2(raw, a):
-                grouped = four.tile([P, N * PACK], BF16, name="woven", align_bytes=ALIGN)
+            def quantize_w2(grouped, raw):
                 nc.scalar.copy(
-                    out=grouped[:].rearrange("p (c i j) -> p c j i", i=PACK, j=PACK),
+                    out=grouped.rearrange("p (c i j) -> p c j i", i=PACK, j=PACK),
                     in_=raw[:].rearrange("p j (c i) -> p c j i", i=PACK),
                 )
-                return quantize(grouped[:], N, two, "w2")
+                return quantize(grouped, N, two, "w2")
 
             def load_table_words(g):
                 words = big.tile([P, T], I32, name="big")
@@ -120,16 +118,18 @@ def tile_list_swipe_swap_scores_kernel(
 
             list1 = load_list(offs, "list1")
             w1q = {}
-            raw = load_weight(w1, 0, slice(0, PASS))
-            w1q[0, 0] = quantize_w1(raw, 0, 0)
+            raw = load_weight(w1, 0, slice(0, PASS), "raw1")
+            grouped = four.tile([P, PASS * PACK], BF16, name="woven", align_bytes=ALIGN)
+            w1q[0, 0] = quantize_w1(nc.vector.tensor_copy, grouped[:], raw)
             words0 = load_table_words(0)
             for quad in range(4):
                 nc.sync.dma_start(
                     out=table_scales[32 * quad : 32 * quad + 8, :].bitcast(I32),
                     in_=tab_scales[:, 4 * quad : 4 * quad + 4, :].bitcast(I32),
                 )
-            raw = load_weight(w1, 1, slice(0, PASS))
-            w1q[0, 1] = quantize_w1(raw, 0, 1)
+            raw = load_weight(w1, 1, slice(0, PASS), "raw1")
+            grouped = four.tile([P, PASS * PACK], BF16, name="woven", align_bytes=ALIGN)
+            w1q[0, 1] = quantize_w1(nc.vector.tensor_copy, grouped[:], raw)
             words1 = load_table_words(1)
             v_codes = [gather_table(words0[:].bitcast(U32), U32, "v0")]
             v_scales = gather_table(table_scales[:], U8, "vs")
@@ -147,8 +147,10 @@ def tile_list_swipe_swap_scores_kernel(
             for s in range(1, PACK):
                 pages[s] = load_page(*slices[s])
                 dealt[s] = load_wgs(s)
-            for g in range(K // PASS):
-                raws[g] = load_weight(w1, g, slice(PASS, 2 * PASS))
+                if s == 1:
+                    for g in range(K // PASS):
+                        raws[g] = load_weight(w1, g, slice(PASS, 2 * PASS), "raw1")
+            raws2 = [load_weight(w2, g, slice(0, N), "raw2") for g in range(H // PASS)]
             pages[PACK] = load_page(*slices[PACK])
             pages[PACK + 1] = load_page(*slices[PACK + 1])
             w4_codes = keep.tile([P, H // PASS, 2 * N], U8, name="w4_codes", align_bytes=ALIGN)
@@ -166,7 +168,7 @@ def tile_list_swipe_swap_scores_kernel(
                 nc.vector.tensor_scalar(turns, y[:], 1.0 / TURN, phase, ALU.mult, ALU.add)
                 nc.vector.scalar_tensor_tensor(angle, turns, -TURN, y[:], ALU.mult, ALU.add)
 
-            def features(psum, s):
+            def features(psum, s, sizes):
                 a, t = slices[s]
                 feature = two.tile([P, S], F32, name="feature")
                 turns = two.tile([P, S], U32, name="turns", align_bytes=ALIGN)
@@ -188,7 +190,7 @@ def tile_list_swipe_swap_scores_kernel(
                                 start=(g == 0),
                                 stop=(g == K // PASS - 1),
                             )
-                    size = five.tile([P, BANK], F32, name="size")
+                    size = sizes[h]
                     nc.scalar.activation(out=size[:], in_=xt[:], func=ACT.Abs)
                     whole_turns(turns[:, half], size)
                     back = five.tile([P, BANK], F32, name="back")
@@ -209,6 +211,7 @@ def tile_list_swipe_swap_scores_kernel(
                 feature = two.tile([P, S], F32, name="feature")
                 turns = two.tile([P, S], I32, name="turns", align_bytes=ALIGN)
                 cosine = two.tile([P, S], F32, name="cosine", align_bytes=ALIGN)
+                angles = []
                 for h in halves:
                     half = slice(h * BANK, (h + 1) * BANK)
                     x = psum.tile([P, BANK], F32, name="xt")
@@ -225,9 +228,10 @@ def tile_list_swipe_swap_scores_kernel(
                         )
                     angle = five.tile([P, BANK], F32, name="size")
                     reduce_on_vector(angle[:], turns[:, half], x, QUARTER)
-                    nc.scalar.activation(out=feature[:, half], in_=angle[:], func=ACT.Sin, bias=TURN * QUARTER)
-                nc.scalar.activation(out=cosine[:], in_=dealt[0][:], func=ACT.Copy, scale=gain_col[:, 0, 0:1])
-                return feature, cosine
+                    nc.scalar.activation(out=cosine[:, half], in_=angle[:], func=ACT.Sin, bias=TURN * QUARTER)
+                    nc.scalar.activation(out=feature[:, half], in_=cosine[:, half], func=ACT.Copy, scale=gain_col[:, 0, 0:1])
+                    angles.append(angle)
+                return feature, angles
 
             def spread(wide, col, s):
                 a, t = slices[s]
@@ -267,24 +271,30 @@ def tile_list_swipe_swap_scores_kernel(
             w2q = {}
             last = len(slices) - 1
             with tc.psum_pool(name="stage1", bufs=2) as psum:
-                place(pages[0], *first_features(psum))
+                feature, sizes = first_features(psum)
+                place(pages[0], feature, dealt[0])
                 parked = {}
                 for s, (a, t) in enumerate(slices):
                     if s < last - 1:
-                        feature, spent, free = features(psum, s + 1)
+                        if s > 0:
+                            sizes = [five.tile([P, BANK], F32, name="size") for h in halves]
+                        feature, spent, free = features(psum, s + 1, sizes)
                         place(pages[s + 1], feature, dealt[(s + 1) % PACK])
                         spent = [tile[:] for tile in spent]
                     else:
                         spent = [five.tile([P, BANK], F32, name=name)[:] for name in ("size", "back", "size", "back")[2 * (s - last + 1) :]]
-                    if s < K // PASS:
-                        w1q[1, s] = quantize_w1(raws[s], 1, s)
-                    elif s < PACK:
-                        w2q[s - 2] = quantize_w2(load_weight(w2, s - 2, slice(0, N)), s - 2)
+                    if s == 1:
+                        for g, grouped in enumerate(free):
+                            w1q[1, g] = quantize_w1(nc.scalar.copy, grouped, raws[g])
+                    if s == 2:
+                        for g, grouped in enumerate(free):
+                            w2q[g] = quantize_w2(grouped[:, 0 : N * PACK], raws2[g])
                     if s == last - 2:
                         for c, woven in enumerate(free):
                             page_q[0, c] = quantize(weave(woven, parked[0], c, PACK), BANK, eight, "mx")
                     if s == last:
-                        feature, unused, free = features(psum, s)
+                        sizes = [five.tile([P, BANK], F32, name="size") for h in halves]
+                        feature, unused, free = features(psum, s, sizes)
                         for u, woven in enumerate(free):
                             page_q[0, 2 + u] = quantize(weave(woven, parked[0], 2 + u, PACK), BANK, eight, "mx")
                         place(pages[s], feature, dealt[t])
@@ -336,19 +346,22 @@ def tile_list_swipe_swap_scores_kernel(
                             stop=(a == H // PASS - 1),
                         )
                     turns1 = three.tile([P, BANK], I32, name="turns1")
-                    nc.vector.tensor_scalar(turns1[:], y1[:], 1.0 / TURN, None, ALU.mult)
                     angle1 = three.tile([P, BANK], F32, name="angle1")
-                    nc.vector.scalar_tensor_tensor(angle1[:], turns1[:], -TURN, y1[:], ALU.mult, ALU.add)
+                    reduce_on_vector(angle1[:], turns1[:], y1, 0.0)
                     sine = three.tile([P, BANK], F32, name="sine")
                     nc.scalar.activation(out=sine[:], in_=angle1[:], func=ACT.Sin)
-                    size = five.tile([P, BANK], F32, name="size")
-                    nc.scalar.activation(out=size[:], in_=y2[:], func=ACT.Abs)
-                    turns2 = three.tile([P, BANK], U32, name="turns2")
-                    whole_turns(turns2[:], size)
                     angle2 = five.tile([P, BANK], F32, name="back")
-                    nc.vector.scalar_tensor_tensor(angle2[:], turns2[:].bitcast(I32), -TURN, size[:], ALU.mult, ALU.add)
+                    if i == 0:
+                        turns2 = three.tile([P, BANK], I32, name="turns2")
+                        reduce_on_vector(angle2[:], turns2[:], y2, QUARTER)
+                    else:
+                        size = five.tile([P, BANK], F32, name="size")
+                        nc.scalar.activation(out=size[:], in_=y2[:], func=ACT.Abs)
+                        turns2 = three.tile([P, BANK], U32, name="turns2")
+                        whole_turns(turns2[:], size)
+                        nc.vector.scalar_tensor_tensor(angle2[:], turns2[:].bitcast(I32), -TURN, size[:], ALU.mult, ALU.add)
                     cos2 = three.tile([P, BANK], F32, name="cos2")
                     nc.scalar.activation(out=cos2[:], in_=angle2[:], func=ACT.Sin, bias=TURN * QUARTER)
                     score = three.tile([P, BANK], F32, name="score")
-                    nc.vector.tensor_tensor(score[:], sine[:], cos2[:], ALU.mult)
+                    nc.gpsimd.tensor_tensor(score[:], sine[:], cos2[:], ALU.mult)
                     nc.sync.dma_start(out=out[cols, c * BANK : (c + 1) * BANK], in_=score[:])

@@ -85,6 +85,13 @@ def tile_list_swipe_swap_scores_kernel(
                 nc.sync.dma_start(out=words[:], in_=tab_words[g].rearrange("p n i -> p (n i)").bitcast(I32))
                 return words
 
+            def load_table_scales(g):
+                for quad in range(4):
+                    nc.sync.dma_start(
+                        out=table_scales[32 * quad + 4 * g : 32 * quad + 4 * g + 4, :].bitcast(I32),
+                        in_=tab_scales[g, 4 * quad : 4 * quad + 4, :].bitcast(I32),
+                    )
+
             def gather_table(src, dtype, name):
                 picked = []
                 for h in halves:
@@ -97,7 +104,7 @@ def tile_list_swipe_swap_scores_kernel(
             def load_wgs(t):
                 dealt = early1.tile([P, S], F32, name="wgs_%d" % t)
                 rows = wgs.rearrange("(q t) j -> t q j", t=PACK)[t]
-                for quad in range(4):
+                for quad in (0, 2, 1, 3):
                     nc.sync.dma_start(out=dealt[32 * quad : 32 * (quad + 1), :], in_=rows)
                 return dealt
 
@@ -121,15 +128,12 @@ def tile_list_swipe_swap_scores_kernel(
             raw = load_weight(w1, 0, slice(0, PASS), "raw1")
             grouped = four.tile([P, PASS * PACK], BF16, name="woven", align_bytes=ALIGN)
             w1q[0, 0] = quantize_w1(nc.vector.tensor_copy, grouped[:], raw)
-            words0 = load_table_words(0)
-            for quad in range(4):
-                nc.sync.dma_start(
-                    out=table_scales[32 * quad : 32 * quad + 8, :].bitcast(I32),
-                    in_=tab_scales[:, 4 * quad : 4 * quad + 4, :].bitcast(I32),
-                )
+            load_table_scales(0)
             raw = load_weight(w1, 1, slice(0, PASS), "raw1")
             grouped = four.tile([P, PASS * PACK], BF16, name="woven", align_bytes=ALIGN)
             w1q[0, 1] = quantize_w1(nc.vector.tensor_copy, grouped[:], raw)
+            words0 = load_table_words(0)
+            load_table_scales(1)
             words1 = load_table_words(1)
             v_codes = [gather_table(words0[:].bitcast(U32), U32, "v0")]
             v_scales = gather_table(table_scales[:], U8, "vs")
@@ -286,7 +290,7 @@ def tile_list_swipe_swap_scores_kernel(
                     if s == 1:
                         for g, grouped in enumerate(free):
                             w1q[1, g] = quantize_w1(nc.scalar.copy, grouped, raws[g])
-                    if s == 2:
+                    if s == 3:
                         for g, grouped in enumerate(free):
                             w2q[g] = quantize_w2(grouped[:, 0 : N * PACK], raws2[g])
                     if s == last - 2:
@@ -314,7 +318,7 @@ def tile_list_swipe_swap_scores_kernel(
         with tc.psum_pool(name="stage2", bufs=4) as psum, tc.tile_pool(name="three", bufs=4) as three:
 
             def finish(c):
-                weave_plane(nc.scalar.copy if c in (1, 2) else nc.vector.tensor_copy, woven_last[c], pages[last], c, PACK - 1)
+                weave_plane(nc.scalar.copy if c > 0 else nc.vector.tensor_copy, woven_last[c], pages[last], c, PACK - 1)
                 page_q[1, c] = quantize(woven_last[c][:], BANK, eight, "mx")
 
             finish(0)
@@ -351,17 +355,14 @@ def tile_list_swipe_swap_scores_kernel(
                     sine = three.tile([P, BANK], F32, name="sine")
                     nc.scalar.activation(out=sine[:], in_=angle1[:], func=ACT.Sin)
                     angle2 = five.tile([P, BANK], F32, name="back")
-                    if i == 0:
-                        turns2 = three.tile([P, BANK], I32, name="turns2")
-                        reduce_on_vector(angle2[:], turns2[:], y2, QUARTER)
-                    else:
-                        size = five.tile([P, BANK], F32, name="size")
-                        nc.scalar.activation(out=size[:], in_=y2[:], func=ACT.Abs)
-                        turns2 = three.tile([P, BANK], U32, name="turns2")
-                        whole_turns(turns2[:], size)
-                        nc.vector.scalar_tensor_tensor(angle2[:], turns2[:].bitcast(I32), -TURN, size[:], ALU.mult, ALU.add)
+                    held = five.tile([P, BANK], F32, name="size")
+                    nc.scalar.copy(out=held[:], in_=y2[:])
+                    turns2 = three.tile([P, BANK], I32, name="turns2")
+                    nc.gpsimd.tensor_scalar(turns2[:], held[:], 1.0 / TURN, QUARTER, ALU.mult, ALU.add)
+                    nc.vector.scalar_tensor_tensor(angle2[:], turns2[:], -TURN, y2[:], ALU.mult, ALU.add)
                     cos2 = three.tile([P, BANK], F32, name="cos2")
                     nc.scalar.activation(out=cos2[:], in_=angle2[:], func=ACT.Sin, bias=TURN * QUARTER)
                     score = three.tile([P, BANK], F32, name="score")
-                    nc.gpsimd.tensor_tensor(score[:], sine[:], cos2[:], ALU.mult)
+                    engine = nc.vector if (c, i) == (chunks[-1], N // P - 1) else nc.gpsimd
+                    engine.tensor_tensor(score[:], sine[:], cos2[:], ALU.mult)
                     nc.sync.dma_start(out=out[cols, c * BANK : (c + 1) * BANK], in_=score[:])

@@ -40,7 +40,7 @@ def tile_list_swipe_swap_scores_kernel(
         big = ctx.enter_context(tc.tile_pool(name="big", bufs=2))
         two = ctx.enter_context(tc.tile_pool(name="two", bufs=2))
         four = ctx.enter_context(tc.tile_pool(name="four", bufs=4))
-        five = ctx.enter_context(tc.tile_pool(name="six", bufs=6))
+        five = ctx.enter_context(tc.tile_pool(name="six", bufs=5))
         eight = ctx.enter_context(tc.tile_pool(name="eight", bufs=8))
         with tc.tile_pool(name="early", bufs=2) as early, tc.tile_pool(name="early1", bufs=1) as early1:
 
@@ -85,13 +85,6 @@ def tile_list_swipe_swap_scores_kernel(
                 nc.sync.dma_start(out=words[:], in_=tab_words[g].rearrange("p n i -> p (n i)").bitcast(I32))
                 return words
 
-            def load_table_scales(g):
-                for quad in range(4):
-                    nc.sync.dma_start(
-                        out=table_scales[32 * quad + 4 * g : 32 * quad + 4 * g + 4, :].bitcast(I32),
-                        in_=tab_scales[g, 4 * quad : 4 * quad + 4, :].bitcast(I32),
-                    )
-
             def gather_table(src, dtype, name):
                 picked = []
                 for h in halves:
@@ -128,12 +121,15 @@ def tile_list_swipe_swap_scores_kernel(
             raw = load_weight(w1, 0, slice(0, PASS), "raw1")
             grouped = four.tile([P, PASS * PACK], BF16, name="woven", align_bytes=ALIGN)
             w1q[0, 0] = quantize_w1(nc.vector.tensor_copy, grouped[:], raw)
-            load_table_scales(0)
+            words0 = load_table_words(0)
+            for quad in range(4):
+                nc.sync.dma_start(
+                    out=table_scales[32 * quad : 32 * quad + 8, :].bitcast(I32),
+                    in_=tab_scales[:, 4 * quad : 4 * quad + 4, :].bitcast(I32),
+                )
             raw = load_weight(w1, 1, slice(0, PASS), "raw1")
             grouped = four.tile([P, PASS * PACK], BF16, name="woven", align_bytes=ALIGN)
             w1q[0, 1] = quantize_w1(nc.vector.tensor_copy, grouped[:], raw)
-            words0 = load_table_words(0)
-            load_table_scales(1)
             words1 = load_table_words(1)
             v_codes = [gather_table(words0[:].bitcast(U32), U32, "v0")]
             v_scales = gather_table(table_scales[:], U8, "vs")
@@ -156,7 +152,6 @@ def tile_list_swipe_swap_scores_kernel(
                         raws[g] = load_weight(w1, g, slice(PASS, 2 * PASS), "raw1")
             raws2 = [load_weight(w2, g, slice(0, N), "raw2") for g in range(H // PASS)]
             pages[PACK] = load_page(*slices[PACK])
-            pages[PACK + 1] = load_page(*slices[PACK + 1])
             w4_codes = keep.tile([P, H // PASS, 2 * N], U8, name="w4_codes", align_bytes=ALIGN)
             nc.sync.dma_start(out=w4_codes[:].bitcast(I32), in_=w4_words.bitcast(I32).rearrange("a p w -> p a w"))
             for quad in range(4):
@@ -195,7 +190,7 @@ def tile_list_swipe_swap_scores_kernel(
                                 stop=(g == K // PASS - 1),
                             )
                     size = sizes[h]
-                    nc.scalar.activation(out=size[:], in_=xt[:], func=ACT.Abs)
+                    nc.scalar.activation(out=size, in_=xt[:], func=ACT.Abs)
                     whole_turns(turns[:, half], size)
                     back = five.tile([P, BANK], F32, name="back")
                     nc.scalar.activation(out=back[:], in_=turns[:, half], func=ACT.Copy, scale=-TURN)
@@ -208,7 +203,7 @@ def tile_list_swipe_swap_scores_kernel(
                     nc.scalar.activation(
                         out=feature[:, half], in_=cosine[:, half], func=ACT.Copy, scale=gain_col[:, a, t : t + 1]
                     )
-                    spent.extend([size, back])
+                    spent.append(back[:])
                 return feature, spent, [turns[:].bitcast(BF16), cosine[:].bitcast(BF16)]
 
             def first_features(psum):
@@ -235,17 +230,18 @@ def tile_list_swipe_swap_scores_kernel(
                     nc.scalar.activation(out=cosine[:, half], in_=angle[:], func=ACT.Sin, bias=TURN * QUARTER)
                     nc.scalar.activation(out=feature[:, half], in_=cosine[:, half], func=ACT.Copy, scale=gain_col[:, 0, 0:1])
                     angles.append(angle)
-                return feature, angles
+                return feature, angles, cosine
 
             def spread(wide, col, s):
                 a, t = slices[s]
                 nc.scalar.activation(out=wide, in_=ones[:], func=ACT.Copy, scale=col[:, a, t : t + 1])
                 return wide
 
-            def place(page, cosine, weight):
-                for h in halves:
-                    cols = slice(h * BANK, (h + 1) * BANK)
-                    entries = list2[:, h * BANK // 16 : (h + 1) * BANK // 16]
+            def place(page, cosine, weight, pieces):
+                width = S // pieces
+                for h in range(pieces):
+                    cols = slice(h * width, (h + 1) * width)
+                    entries = list2[:, h * width // 16 : (h + 1) * width // 16]
                     nc.vector.tensor_tensor(page[:].indirect(entries), cosine[:, cols], weight[:, cols], ALU.mult)
 
             def exchange(page, traded, shifted, first, second):
@@ -275,45 +271,44 @@ def tile_list_swipe_swap_scores_kernel(
             w2q = {}
             last = len(slices) - 1
             with tc.psum_pool(name="stage1", bufs=2) as psum:
-                feature, sizes = first_features(psum)
-                place(pages[0], feature, dealt[0])
                 parked = {}
                 for s, (a, t) in enumerate(slices):
-                    if s < last - 1:
-                        if s > 0:
-                            sizes = [five.tile([P, BANK], F32, name="size") for h in halves]
-                        feature, spent, free = features(psum, s + 1, sizes)
-                        place(pages[s + 1], feature, dealt[(s + 1) % PACK])
+                    if s == 0:
+                        feature, spent, cosine = first_features(psum)
                         spent = [tile[:] for tile in spent]
+                        place(pages[s], feature, dealt[t], 2)
                     else:
-                        spent = [five.tile([P, BANK], F32, name=name)[:] for name in ("size", "back", "size", "back")[2 * (s - last + 1) :]]
-                    if s == 1:
+                        if s == 1:
+                            sizes = [cosine[:, h * BANK : (h + 1) * BANK] for h in halves]
+                        else:
+                            sizes = [five.tile([P, BANK], F32, name="size")[:] for h in halves]
+                        feature, spent, free = features(psum, s, sizes)
+                        place(pages[s], feature, dealt[t], 1)
+                    if s == 2:
                         for g, grouped in enumerate(free):
                             w1q[1, g] = quantize_w1(nc.scalar.copy, grouped, raws[g])
-                    if s == 3:
+                    if s == 4:
                         for g, grouped in enumerate(free):
                             w2q[g] = quantize_w2(grouped[:, 0 : N * PACK], raws2[g])
-                    if s == last - 2:
-                        for c, woven in enumerate(free):
+                    if s >= last - 1:
+                        for u, woven in enumerate(free):
+                            c = 2 * (s - last + 1) + u
                             page_q[0, c] = quantize(weave(woven, parked[0], c, PACK), BANK, eight, "mx")
                     if s == last:
-                        sizes = [five.tile([P, BANK], F32, name="size") for h in halves]
-                        feature, unused, free = features(psum, s, sizes)
-                        for u, woven in enumerate(free):
-                            page_q[0, 2 + u] = quantize(weave(woven, parked[0], 2 + u, PACK), BANK, eight, "mx")
-                        place(pages[s], feature, dealt[t])
                         woven_last = [four.tile([P, BANK * PACK], BF16, name="woven", align_bytes=ALIGN) for c in chunks]
                         for c in chunks:
                             weave(woven_last[c][:], parked[1], c, PACK - 1)
-                        spent = [part[:, 0, BANK // 2 : 3 * BANK // 2] for part in parked[1]] + spent
+                        spent = [part[:, 0, BANK // 2 : 3 * BANK // 2] for part in parked[1]]
                     traded, shifted = spread(spent[0], trade_col, s), spread(spent[1], shift_col, s)
-                    exchange(pages[s], traded, shifted, spent[2], spent[3])
+                    first = two.tile([P, PAIRS], F32, name="first")
+                    second = two.tile([P, PAIRS], F32, name="second")
+                    exchange(pages[s], traded, shifted, first[:], second[:])
                     if s < last:
                         if t == 0:
                             parked[a] = [big.tile([P, PACK, T2 // 2], F32, name="big") for u in range(2)]
                         park(pages[s], parked[a], t)
-                        if s + 6 <= last:
-                            pages[s + 6] = load_page(*slices[s + 6])
+                        if s + 5 <= last:
+                            pages[s + 5] = load_page(*slices[s + 5])
 
         with tc.psum_pool(name="stage2", bufs=4) as psum, tc.tile_pool(name="three", bufs=4) as three:
 
@@ -355,14 +350,13 @@ def tile_list_swipe_swap_scores_kernel(
                     sine = three.tile([P, BANK], F32, name="sine")
                     nc.scalar.activation(out=sine[:], in_=angle1[:], func=ACT.Sin)
                     angle2 = five.tile([P, BANK], F32, name="back")
-                    held = five.tile([P, BANK], F32, name="size")
-                    nc.scalar.copy(out=held[:], in_=y2[:])
-                    turns2 = three.tile([P, BANK], I32, name="turns2")
-                    nc.gpsimd.tensor_scalar(turns2[:], held[:], 1.0 / TURN, QUARTER, ALU.mult, ALU.add)
-                    nc.vector.scalar_tensor_tensor(angle2[:], turns2[:], -TURN, y2[:], ALU.mult, ALU.add)
+                    size = five.tile([P, BANK], F32, name="size")
+                    nc.scalar.activation(out=size[:], in_=y2[:], func=ACT.Abs)
+                    turns2 = three.tile([P, BANK], U32, name="turns2")
+                    whole_turns(turns2[:], size)
+                    nc.vector.scalar_tensor_tensor(angle2[:], turns2[:].bitcast(I32), -TURN, size[:], ALU.mult, ALU.add)
                     cos2 = three.tile([P, BANK], F32, name="cos2")
                     nc.scalar.activation(out=cos2[:], in_=angle2[:], func=ACT.Sin, bias=TURN * QUARTER)
                     score = three.tile([P, BANK], F32, name="score")
-                    engine = nc.vector if (c, i) == (chunks[-1], N // P - 1) else nc.gpsimd
-                    engine.tensor_tensor(score[:], sine[:], cos2[:], ALU.mult)
+                    nc.vector.tensor_tensor(score[:], sine[:], cos2[:], ALU.mult)
                     nc.sync.dma_start(out=out[cols, c * BANK : (c + 1) * BANK], in_=score[:])

import math
from contextlib import ExitStack

import concourse.mybir as mybir
from concourse.masks import make_identity

T, S, T2, PAIRS, K, H, N = 4096, 1024, 2048, 512, 1024, 1024, 384
FLOPS = 2 * K * H * S + 2 * 2 * H * N * T2

F32 = mybir.dt.float32
BF16 = mybir.dt.bfloat16
I32 = mybir.dt.int32
U32 = mybir.dt.uint32
U16 = mybir.dt.uint16
U8 = mybir.dt.uint8
E4M3X4 = mybir.dt.float8_e4m3fn_x4
E2M1X4 = mybir.dt.float4_e2m1fn_x4
ACT = mybir.ActivationFunctionType
ALU = mybir.AluOpType

P = 128
PACK = 4
PASS = P * PACK
BANK = 512
TURN = 2.0 * math.pi
QUARTER = 0.25
ALIGN = 64


def tile_list_swipe_swap_scores_kernel(
    tc, tab_words, tab_scales, offs, offs2, offs3, offs4, w1, gain, wgs, page0, trade, shift, w4_words, w4_scales, w2, out
):
    nc = tc.nc
    slices = [(a, t) for a in range(H // PASS) for t in range(PACK)]
    chunks = range(T2 // BANK)
    halves = range(S // BANK)

    with ExitStack() as ctx:
        keep = ctx.enter_context(tc.tile_pool(name="keep", bufs=1))
        big = ctx.enter_context(tc.tile_pool(name="big", bufs=2))
        two = ctx.enter_context(tc.tile_pool(name="two", bufs=2))
        four = ctx.enter_context(tc.tile_pool(name="four", bufs=4))
        five = ctx.enter_context(tc.tile_pool(name="six", bufs=5))
        eight = ctx.enter_context(tc.tile_pool(name="eight", bufs=8))
        with tc.tile_pool(name="early", bufs=2) as early, tc.tile_pool(name="early1", bufs=1) as early1:

            def load_list(src, name):
                lst = keep.tile(list(src.shape), U16, name=name)
                nc.sync.dma_start(lst[:], src)
                return lst

            def load_rows(src, name):
                col = keep.tile([P, H // PASS, PACK], F32, name=name)
                nc.sync.dma_start(out=col[:], in_=src.rearrange("(a p t) -> p a t", p=P, t=PACK))
                return col

            def load_weight(w, g, cols, name):
                width = cols.stop - cols.start
                raw = early.tile([P, PACK, width], F32, name=name)
                nc.sync.dma_start(out=raw[:], in_=w[g * PASS : (g + 1) * PASS, cols].rearrange("(p j) c -> p j c", j=PACK))
                return raw

            def quantize(grouped, width, pool, name):
                codes = pool.tile([P, width], U32, name=name + "_codes", align_bytes=ALIGN)
                scales = pool.tile([P, width], U8, name=name + "_scales", align_bytes=ALIGN)
                nc.vector.quantize_mx(out=codes[:].bitcast(E4M3X4), scales=scales[:], in_=grouped)
                return codes, scales

            def quantize_w1(copy, grouped, raw):
                copy(
                    out=grouped.rearrange("p (t m j) -> p m j t", t=PACK, j=PACK),
                    in_=raw[:].rearrange("p j (m t) -> p m j t", t=PACK),
                )
                return quantize(grouped, PASS, eight, "mx")

            def quantize_w2(grouped, raw):
                nc.scalar.copy(
                    out=grouped.rearrange("p (c i j) -> p c j i", i=PACK, j=PACK),
                    in_=raw[:].rearrange("p j (c i) -> p c j i", i=PACK),
                )
                return quantize(grouped, N, two, "w2")

            def load_table_words(g):
                words = big.tile([P, T], I32, name="big")
                nc.sync.dma_start(out=words[:], in_=tab_words[g].rearrange("p n i -> p (n i)").bitcast(I32))
                return words

            def gather_table(src, dtype, name):
                picked = []
                for h in halves:
                    part = early1.tile([P, BANK], dtype, name="%s_%d" % (name, h), align_bytes=ALIGN)
                    cols = slice(h * BANK // 16, (h + 1) * BANK // 16)
                    nc.vector.tensor_copy(part[:], src.indirect(list1[:, cols]))
                    picked.append(part)
                return picked

            def load_wgs(t):
                dealt = early1.tile([P, S], F32, name="wgs_%d" % t)
                rows = wgs.rearrange("(q t) j -> t q j", t=PACK)[t]
                for quad in (0, 2, 1, 3):
                    nc.sync.dma_start(out=dealt[32 * quad : 32 * (quad + 1), :], in_=rows)
                return dealt

            def load_page(a, t):
                page = five.tile([P, T2], F32, name="page")
                rows = page0[a * PASS : (a + 1) * PASS, :].rearrange("(p t) c -> t p c", t=PACK)[t]
                nc.sync.dma_start(out=page[:], in_=rows)
                return page

            table_scales = early1.tile([P, T], U8, name="table_scales")
            nc.vector.memset(table_scales[:].bitcast(I32), 0)
            ident = keep.tile([P, P], F32, name="ident")
            make_identity(nc, ident[:])
            ones = keep.tile([P, PAIRS], F32, name="ones")
            nc.gpsimd.memset(ones[:], 1.0)
            w4_plane = keep.tile([P, H // PASS, N], U8, name="w4_plane", align_bytes=ALIGN)
            nc.gpsimd.memset(w4_plane[:].rearrange("p a n -> p (a n)").bitcast(I32), 0)

            list1 = load_list(offs, "list1")
            w1q = {}
            raw = load_weight(w1, 0, slice(0, PASS), "raw1")
            grouped = four.tile([P, PASS * PACK], BF16, name="woven", align_bytes=ALIGN)
            w1q[0, 0] = quantize_w1(nc.vector.tensor_copy, grouped[:], raw)
            words0 = load_table_words(0)
            for quad in range(4):
                nc.sync.dma_start(
                    out=table_scales[32 * quad : 32 * quad + 8, :].bitcast(I32),
                    in_=tab_scales[:, 4 * quad : 4 * quad + 4, :].bitcast(I32),
                )
            raw = load_weight(w1, 1, slice(0, PASS), "raw1")
            grouped = four.tile([P, PASS * PACK], BF16, name="woven", align_bytes=ALIGN)
            w1q[0, 1] = quantize_w1(nc.vector.tensor_copy, grouped[:], raw)
            words1 = load_table_words(1)
            v_codes = [gather_table(words0[:].bitcast(U32), U32, "v0")]
            v_scales = gather_table(table_scales[:], U8, "vs")
            v_codes.append(gather_table(words1[:].bitcast(U32), U32, "v1"))

            gain_col = load_rows(gain, "gain_col")
            list2 = load_list(offs2, "list2")
            dealt = {0: load_wgs(0)}
            pages = {0: load_page(*slices[0])}
            list3 = load_list(offs3, "list3")
            list4 = load_list(offs4, "list4")
            trade_col = load_rows(trade, "trade_col")
            shift_col = load_rows(shift, "shift_col")
            raws = {}
            for s in range(1, PACK):
                pages[s] = load_page(*slices[s])
                dealt[s] = load_wgs(s)
                if s == 1:
                    for g in range(K // PASS):
                        raws[g] = load_weight(w1, g, slice(PASS, 2 * PASS), "raw1")
            raws2 = [load_weight(w2, g, slice(0, N), "raw2") for g in range(H // PASS)]
            pages[PACK] = load_page(*slices[PACK])
            w4_codes = keep.tile([P, H // PASS, 2 * N], U8, name="w4_codes", align_bytes=ALIGN)
            nc.sync.dma_start(out=w4_codes[:].bitcast(I32), in_=w4_words.bitcast(I32).rearrange("a p w -> p a w"))
            for quad in range(4):
                nc.sync.dma_start(
                    out=w4_plane[32 * quad : 32 * quad + 4, :, :].bitcast(I32),
                    in_=w4_scales[:, 4 * quad : 4 * quad + 4, :].bitcast(I32).rearrange("a q w -> q a w"),
                )

            def whole_turns(turns, size):
                nc.scalar.activation(out=turns, in_=size[:], func=ACT.Copy, scale=1.0 / TURN, bias=QUARTER)

            def reduce_on_vector(angle, turns, y, phase):
                nc.vector.tensor_scalar(turns, y[:], 1.0 / TURN, phase, ALU.mult, ALU.add)
                nc.vector.scalar_tensor_tensor(angle, turns, -TURN, y[:], ALU.mult, ALU.add)

            def features(psum, s, sizes):
                a, t = slices[s]
                feature = two.tile([P, S], F32, name="feature")
                turns = two.tile([P, S], U32, name="turns", align_bytes=ALIGN)
                cosine = two.tile([P, S], F32, name="cosine", align_bytes=ALIGN)
                spent = []
                for h in halves:
                    half = slice(h * BANK, (h + 1) * BANK)
                    xt = psum.tile([P, BANK], F32, name="xt")
                    for i in range(BANK // P):
                        cols = slice(i * P, (i + 1) * P)
                        for g in range(K // PASS):
                            codes, scales = w1q[a, g]
                            nc.tensor.matmul_mx(
                                out=xt[:, cols],
                                lhsT=v_codes[g][h][:, cols].bitcast(E4M3X4),
                                lhsT_scale=v_scales[h][4 * g :, cols],
                                rhs=codes[:, t * P : (t + 1) * P].bitcast(E4M3X4),
                                rhs_scale=scales[:, t * P : (t + 1) * P],
                                start=(g == 0),
                                stop=(g == K // PASS - 1),
                            )
                    size = sizes[h]
                    nc.scalar.activation(out=size, in_=xt[:], func=ACT.Abs)
                    whole_turns(turns[:, half], size)
                    back = five.tile([P, BANK], F32, name="back")
                    nc.scalar.activation(out=back[:], in_=turns[:, half], func=ACT.Copy, scale=-TURN)
                    angle = psum.tile([P, BANK], F32, name="angle")
                    for i in range(BANK // P):
                        cols = slice(i * P, (i + 1) * P)
                        nc.tensor.matmul(angle[:, cols], size[:, cols], ident[:], start=True, stop=False, is_transpose=True)
                        nc.tensor.matmul(angle[:, cols], back[:, cols], ident[:], start=False, stop=True, is_transpose=True)
                    nc.scalar.activation(out=cosine[:, half], in_=angle[:], func=ACT.Sin, bias=TURN * QUARTER)
                    nc.scalar.activation(
                        out=feature[:, half], in_=cosine[:, half], func=ACT.Copy, scale=gain_col[:, a, t : t + 1]
                    )
                    spent.append(back[:])
                return feature, spent, [turns[:].bitcast(BF16), cosine[:].bitcast(BF16)]

            def first_features(psum):
                feature = two.tile([P, S], F32, name="feature")
                turns = two.tile([P, S], I32, name="turns", align_bytes=ALIGN)
                cosine = two.tile([P, S], F32, name="cosine", align_bytes=ALIGN)
                angles = []
                for h in halves:
                    half = slice(h * BANK, (h + 1) * BANK)
                    x = psum.tile([P, BANK], F32, name="xt")
                    for g in range(K // PASS):
                        codes, scales = w1q[0, g]
                        nc.tensor.matmul_mx(
                            out=x[:],
                            lhsT=codes[:, 0:P].bitcast(E4M3X4),
                            lhsT_scale=scales[:, 0:P],
                            rhs=v_codes[g][h][:].bitcast(E4M3X4),
                            rhs_scale=v_scales[h][4 * g :, :],
                            start=(g == 0),
                            stop=(g == K // PASS - 1),
                        )
                    angle = five.tile([P, BANK], F32, name="size")
                    reduce_on_vector(angle[:], turns[:, half], x, QUARTER)
                    nc.scalar.activation(out=cosine[:, half], in_=angle[:], func=ACT.Sin, bias=TURN * QUARTER)
                    nc.scalar.activation(out=feature[:, half], in_=cosine[:, half], func=ACT.Copy, scale=gain_col[:, 0, 0:1])
                    angles.append(angle)
                return feature, angles, cosine

            def spread(wide, col, s):
                a, t = slices[s]
                nc.scalar.activation(out=wide, in_=ones[:], func=ACT.Copy, scale=col[:, a, t : t + 1])
                return wide

            def place(page, cosine, weight, pieces):
                width = S // pieces
                for h in range(pieces):
                    cols = slice(h * width, (h + 1) * width)
                    entries = list2[:, h * width // 16 : (h + 1) * width // 16]
                    nc.vector.tensor_tensor(page[:].indirect(entries), cosine[:, cols], weight[:, cols], ALU.mult)

            def exchange(page, traded, shifted, first, second):
                nc.vector.tensor_copy(second, page[:].indirect(list4[:]))
                nc.vector.tensor_copy(first, page[:].indirect(list3[:]))
                nc.vector.tensor_tensor(page[:].indirect(list3[:]), second, traded, ALU.mult)
                nc.vector.tensor_tensor(page[:].indirect(list4[:]), first, shifted, ALU.add)

            def park(page, parked, t):
                for u, part in enumerate(parked):
                    nc.sync.dma_start(out=part[:, t, :], in_=page[:, u * T2 // 2 : (u + 1) * T2 // 2])

            def weave(woven, parked, c, planes):
                src = parked[c // 2][:, 0:planes, (c % 2) * BANK : (c % 2 + 1) * BANK]
                nc.scalar.copy(
                    out=woven.rearrange("p (c i t) -> p c t i", i=PACK, t=PACK)[:, :, 0:planes, :],
                    in_=src.rearrange("p t (c i) -> p c t i", i=PACK),
                )
                return woven

            def weave_plane(copy, woven, page, c, t):
                copy(
                    out=woven[:].rearrange("p (c t) -> p c t", t=PACK)[:, :, t], in_=page[:, c * BANK : (c + 1) * BANK]
                )

            page_q = {}
            w2q = {}
            last = len(slices) - 1
            with tc.psum_pool(name="stage1", bufs=2) as psum:
                parked = {}
                for s, (a, t) in enumerate(slices):
                    if s == 0:
                        feature, spent, cosine = first_features(psum)
                        spent = [tile[:] for tile in spent]
                        place(pages[s], feature, dealt[t], 2)
                    else:
                        if s == 1:
                            sizes = [cosine[:, h * BANK : (h + 1) * BANK] for h in halves]
                        else:
                            sizes = [five.tile([P, BANK], F32, name="size")[:] for h in halves]
                        feature, spent, free = features(psum, s, sizes)
                        place(pages[s], feature, dealt[t], 1)
                    if s == 2:
                        for g, grouped in enumerate(free):
                            w1q[1, g] = quantize_w1(nc.scalar.copy, grouped, raws[g])
                    if s == 4:
                        for g, grouped in enumerate(free):
                            w2q[g] = quantize_w2(grouped[:, 0 : N * PACK], raws2[g])
                    if s >= last - 1:
                        for u, woven in enumerate(free):
                            c = 2 * (s - last + 1) + u
                            page_q[0, c] = quantize(weave(woven, parked[0], c, PACK), BANK, eight, "mx")
                    if s == last:
                        woven_last = [four.tile([P, BANK * PACK], BF16, name="woven", align_bytes=ALIGN) for c in chunks]
                        for c in chunks:
                            weave(woven_last[c][:], parked[1], c, PACK - 1)
                        spent = [part[:, 0, BANK // 2 : 3 * BANK // 2] for part in parked[1]]
                    traded, shifted = spread(spent[0], trade_col, s), spread(spent[1], shift_col, s)
                    first = two.tile([P, PAIRS], F32, name="first")
                    second = two.tile([P, PAIRS], F32, name="second")
                    exchange(pages[s], traded, shifted, first[:], second[:])
                    if s < last:
                        if t == 0:
                            parked[a] = [big.tile([P, PACK, T2 // 2], F32, name="big") for u in range(2)]
                        park(pages[s], parked[a], t)
                        if s + 5 <= last:
                            pages[s + 5] = load_page(*slices[s + 5])

        with tc.psum_pool(name="stage2", bufs=4) as psum, tc.tile_pool(name="three", bufs=4) as three:

            def finish(c):
                weave_plane(nc.scalar.copy if c > 0 else nc.vector.tensor_copy, woven_last[c], pages[last], c, PACK - 1)
                page_q[1, c] = quantize(woven_last[c][:], BANK, eight, "mx")

            finish(0)
            for c in chunks:
                if c + 1 in chunks:
                    finish(c + 1)
                for i in range(N // P):
                    cols = slice(i * P, (i + 1) * P)
                    y1 = psum.tile([P, BANK], F32, name="y1")
                    y2 = psum.tile([P, BANK], F32, name="y2")
                    for a in range(H // PASS):
                        codes, scales = page_q[a, c]
                        nc.tensor.matmul_mx(
                            out=y1[:],
                            lhsT=w4_codes[:, a, 2 * i * P : 2 * (i + 1) * P].bitcast(E2M1X4),
                            lhsT_scale=w4_plane[:, a, cols],
                            rhs=codes[:].bitcast(E4M3X4),
                            rhs_scale=scales[:],
                            start=(a == 0),
                            stop=(a == H // PASS - 1),
                        )
                        nc.tensor.matmul_mx(
                            out=y2[:],
                            lhsT=w2q[a][0][:, cols].bitcast(E4M3X4),
                            lhsT_scale=w2q[a][1][:, cols],
                            rhs=codes[:].bitcast(E4M3X4),
                            rhs_scale=scales[:],
                            start=(a == 0),
                            stop=(a == H // PASS - 1),
                        )
                    turns1 = three.tile([P, BANK], I32, name="turns1")
                    angle1 = three.tile([P, BANK], F32, name="angle1")
                    reduce_on_vector(angle1[:], turns1[:], y1, 0.0)
                    sine = three.tile([P, BANK], F32, name="sine")
                    nc.scalar.activation(out=sine[:], in_=angle1[:], func=ACT.Sin)
                    angle2 = five.tile([P, BANK], F32, name="back")
                    size = five.tile([P, BANK], F32, name="size")
                    nc.scalar.activation(out=size[:], in_=y2[:], func=ACT.Abs)
                    turns2 = three.tile([P, BANK], U32, name="turns2")
                    whole_turns(turns2[:], size)
                    nc.vector.scalar_tensor_tensor(angle2[:], turns2[:].bitcast(I32), -TURN, size[:], ALU.mult, ALU.add)
                    cos2 = three.tile([P, BANK], F32, name="cos2")
                    nc.scalar.activation(out=cos2[:], in_=angle2[:], func=ACT.Sin, bias=TURN * QUARTER)
                    score = three.tile([P, BANK], F32, name="score")
                    nc.vector.tensor_tensor(score[:], sine[:], cos2[:], ALU.mult)
                    nc.sync.dma_start(out=out[cols, c * BANK : (c + 1) * BANK], in_=score[:])
